import numpy as np
import ml_dtypes


def mxq(x, axis, fmt="e4m3"):
    dtype, down = {"e4m3": (ml_dtypes.float8_e4m3fn, 7), "e5m2": (ml_dtypes.float8_e5m2, 14)}[fmt]
    v = np.moveaxis(np.asarray(x, np.float32).astype(ml_dtypes.bfloat16).astype(np.float64), axis, -1)
    blocks = v.reshape(v.shape[:-1] + (-1, 32))
    amax = np.abs(blocks).max(-1, keepdims=True)
    byte = np.maximum(np.where(amax > 0, np.frexp(amax)[1] - 1 + 127, 0) - down, 1)
    scale = np.exp2(byte - 127.0)
    codes = (blocks / scale).astype(np.float32).astype(dtype).astype(np.float64)
    return np.moveaxis((codes * scale).reshape(v.shape), -1, axis)


WIDE = False


def mx_kscale(k):
    if not WIDE:
        return np.ones(k)
    levels = np.array([30, -30])
    if k % 512:
        return np.exp2(np.random.permutation(np.resize(levels, k // 32))).repeat(32)
    a = np.empty((k // 512, 16))
    for p in range(k // 512):
        a[p, :8] = np.random.permutation(np.resize(levels, 8))
        for g in range(8):
            far = levels[np.abs(levels - a[p, g]) >= 10]
            a[p, g + 8] = far[np.random.randint(len(far))]
    return np.exp2(a.ravel()).repeat(32)


def f64(x):
    return np.asarray(x).astype(np.float64)


def striped(idx):
    return np.tile(np.asarray(idx).reshape(-1, 16).T, (8, 1)).astype(np.uint16)


def unstriped(offs):
    return offs[:16].T.reshape(-1).astype(np.int64)


E2M1 = np.array([0.0, 0.5, 1.0, 1.5, 2.0, 3.0, 4.0, 6.0, -0.0, -0.5, -1.0, -1.5, -2.0, -3.0, -4.0, -6.0])


def pack_weight(w, fmt):
    k, n = w.shape
    w = f64(np.asarray(w, np.float32).astype(ml_dtypes.bfloat16)).reshape(k // 32, 32, n)
    amax = np.abs(w).max(1)
    if fmt in ("e4m3", "e5m2"):
        byte = np.frexp(amax)[1] - 1 + 127 - (7 if fmt == "e4m3" else 14)
    else:
        mant, ex = np.frexp(amax / 6.0)
        byte = np.where(mant > 0.5, ex, ex - 1) + 127
    byte = np.clip(np.where(amax > 0, byte, 1), 1, 254)
    scaled = (w * np.exp2(127.0 - byte)[:, None, :]).reshape(k, n).astype(np.float32)
    by_word = np.ascontiguousarray(scaled.reshape(k // 512, 128, 4, n).transpose(0, 1, 3, 2))
    if fmt in ("e4m3", "e5m2"):
        words = by_word.astype(ml_dtypes.float8_e4m3fn if fmt == "e4m3" else ml_dtypes.float8_e5m2).view(np.uint8)
    else:
        c = by_word.astype(ml_dtypes.float4_e2m1fn).view(np.uint8) & 0xF
        words = (c[..., 0::2] | (c[..., 1::2] << 4)).reshape(k // 512, 128, 2 * n)
    return np.ascontiguousarray(words), np.ascontiguousarray(byte.astype(np.uint8).reshape(k // 512, 16, n))


def unpack_weight(words, scales, fmt):
    g, _, n = scales.shape
    words = np.ascontiguousarray(words).reshape(g, 128, n, -1)
    if fmt in ("e4m3", "e5m2"):
        vals = words.view(ml_dtypes.float8_e4m3fn if fmt == "e4m3" else ml_dtypes.float8_e5m2).astype(np.float64)
    else:
        nib = np.empty((g, 128, n, 4), np.uint8)
        nib[..., 0::2] = words & 0xF
        nib[..., 1::2] = words >> 4
        vals = E2M1[nib]
    vals = vals * np.repeat(np.exp2(scales.astype(np.float64) - 127.0), 8, axis=1)[..., None]
    return vals.transpose(0, 1, 3, 2).reshape(g * 512, n)


K, T, J, S, R, F, Z, N = 512, 512, 256, 512, 512, 512, 1024, 256


def setup_inputs():
    n = np.random.standard_normal
    idx = np.random.permutation(T)[:J]
    idx2 = np.random.permutation(S)[:J]
    idx3 = np.random.permutation(Z)[:J]
    fk = mx_kscale(K)
    fr = mx_kscale(R)
    ff = mx_kscale(F)
    wp = pack_weight(n((K, R)) * 1 / np.sqrt(K) * fk[:, None] * fr, "e2m1")
    xop = pack_weight(n((F, Z)) / ff[:, None], "e5m2")
    w2p = pack_weight(n((F, R)) * 1 / np.sqrt(F) * ff[:, None] * fr, "e2m1")
    wbp = pack_weight(n((R, N)) * 1 / np.sqrt(R) / fr[:, None], "e2m1")
    return {
        "xa": (n((K, T))).astype(np.float32),
        "xb": (n((K, S))).astype(np.float32),
        "hb": (np.random.uniform(0.2, 0.9, (K, 1))).astype(np.float32),
        "fk": (np.random.uniform(0.5, 2.0, (K, 1)) / fk[:, None]).astype(np.float32),
        "w_words": wp[0],
        "w_scales": wp[1],
        "xo_words": xop[0],
        "xo_scales": xop[1],
        "w2_words": w2p[0],
        "w2_scales": w2p[1],
        "wb_words": wbp[0],
        "wb_scales": wbp[1],
        "rs": (1.0 * n((J, N))).astype(np.float32),
        "offs": striped(idx),
        "offs2": striped(idx2),
        "offs3": striped(idx3),
    }


def reference(xa, xb, hb, fk, w_words, w_scales, xo_words, xo_scales, w2_words, w2_scales, wb_words, wb_scales, rs, offs, offs2, offs3):
    idx = unstriped(offs)
    idx2 = unstriped(offs2)
    idx3 = unstriped(offs3)
    wu = unpack_weight(w_words, w_scales, "e2m1")
    xou = unpack_weight(xo_words, xo_scales, "e5m2")
    w2u = unpack_weight(w2_words, w2_scales, "e2m1")
    wbu = unpack_weight(wb_words, wb_scales, "e2m1")
    u = (f64(xa)[:, idx] - np.minimum(f64(xb)[:, idx2], f64(hb))) * f64(fk)
    uq = mxq(u, 0, "e4m3")
    a = wu.T @ uq
    xoidx3g = xou[:, idx3]
    q = w2u.T @ xoidx3g
    y1 = np.pad(q, ((0, 0), (1, 0)))[:, :J]
    hid = np.maximum(a, q - 0.6 * y1)
    hidq = mxq(hid, 0, "e5m2")
    p = hidq.T @ wbu
    pk2 = np.max(np.abs(p), axis=1, keepdims=True)
    y = p / (pk2 + 0.2) + 0.3 * f64(rs)
    return y

@@ -1,0 +1,203 @@
+from contextlib import ExitStack
+
+import concourse.mybir as mybir
+
+K, T, J, S, R, F, Z, N = 512, 512, 256, 512, 512, 512, 1024, 256
+FLOPS = 2 * K * R * J + 2 * F * R * J + 2 * R * J * N
+
+F32 = mybir.dt.float32
+BF16 = mybir.dt.bfloat16
+I32 = mybir.dt.int32
+U32 = mybir.dt.uint32
+U16 = mybir.dt.uint16
+U8 = mybir.dt.uint8
+E4M3 = mybir.dt.float8_e4m3fn_x4
+E5M2 = mybir.dt.float8_e5m2_x4
+E2M1 = mybir.dt.float4_e2m1fn_x4
+ALU = mybir.AluOpType
+ACT = mybir.ActivationFunctionType
+
+P = 128
+PACK = 4
+HALF = 128
+HALVES = J // HALF
+
+
+def load_scale_rows(queue, plane, scales):
+    for quad in range(4):
+        queue.dma_start(
+            out=plane[32 * quad : 32 * quad + 4, :].bitcast(I32),
+            in_=scales[0, 4 * quad : 4 * quad + 4, :].bitcast(I32),
+        )
+
+
+def deal_columns(nc, dealt, raw, run):
+    nc.vector.tensor_copy(
+        out=dealt.rearrange("p (t c i) -> p c t i", t=PACK, i=run),
+        in_=raw.rearrange("p (c i t) -> p c t i", t=PACK, i=run),
+    )
+
+
+def tile_list_two_boundedgaps_other_stepgap_rowpeaks_kernel(
+    tc, xa, xb, hb, fk, w_words, w_scales, xo_words, xo_scales, w2_words, w2_scales,
+    wb_words, wb_scales, rs, offs, offs2, offs3, out,
+):
+    nc = tc.nc
+    with ExitStack() as ctx:
+        sb = ctx.enter_context(tc.tile_pool(name="sb", bufs=1))
+        ps = ctx.enter_context(tc.psum_pool(name="ps", bufs=1))
+
+        def tile(name, shape, dtype):
+            return sb.tile(shape, dtype, name=name, align_bytes=64)
+
+        list_a = tile("list_a", [P, J // 16], U16)
+        list_b = tile("list_b", [P, J // 16], U16)
+        list_o = tile("list_o", [P, J // 16], U16)
+        xo_table = tile("xo_table", [P, Z], I32)
+        xo_plane = tile("xo_plane", [P, Z], U8)
+        w_raw = tile("w_raw", [P, 2 * R], U8)
+        w_plane_raw = tile("w_plane_raw", [P, R], U8)
+        w2_raw = tile("w2_raw", [P, 2 * R], U8)
+        w2_plane_raw = tile("w2_plane_raw", [P, R], U8)
+        wb_codes = tile("wb_codes", [P, 2 * N], U8)
+        wb_plane = tile("wb_plane", [P, N], U8)
+        xa_pairs = [tile("xa_pair%d" % i, [P, 2, T], F32) for i in range(2)]
+        xb_pairs = [tile("xb_pair%d" % i, [P, 2, S], F32) for i in range(2)]
+        bound = tile("bound", [P, PACK], F32)
+        factor = tile("factor", [P, PACK], F32)
+        neg_factor = tile("neg_factor", [P, PACK], F32)
+        resid = tile("resid", [P, HALVES, N], F32)
+        prev_q = tile("prev_q", [P, J, PACK], F32)
+
+        for plane in (xo_plane, w2_plane_raw, w_plane_raw, wb_plane):
+            nc.vector.memset(plane[:].bitcast(I32), 0)
+        nc.vector.memset(prev_q[:, 0, :], 0.0)
+
+        xa_rows = xa.rearrange("(p t) c -> p t c", t=PACK)
+        xb_rows = xb.rearrange("(p t) c -> p t c", t=PACK)
+        nc.sync.dma_start(list_b[:], offs2)
+        nc.sync.dma_start(out=xb_pairs[0][:], in_=xb_rows[:, 0:2, :])
+        nc.sync.dma_start(list_o[:], offs3)
+        nc.sync.dma_start(out=xo_table[:], in_=xo_words[0].rearrange("p n t -> p (n t)").bitcast(I32))
+        load_scale_rows(nc.scalar, xo_plane, xo_scales)
+        nc.sync.dma_start(list_a[:], offs)
+        nc.sync.dma_start(out=xa_pairs[0][:], in_=xa_rows[:, 0:2, :])
+        nc.sync.dma_start(out=w2_raw[:].bitcast(I32), in_=w2_words[0].bitcast(I32))
+        load_scale_rows(nc.sync, w2_plane_raw, w2_scales)
+        nc.sync.dma_start(out=bound[:], in_=hb.rearrange("(p t) o -> p (t o)", t=PACK))
+        nc.sync.dma_start(out=xb_pairs[1][:], in_=xb_rows[:, 2:4, :])
+        nc.sync.dma_start(out=xa_pairs[1][:], in_=xa_rows[:, 2:4, :])
+        nc.sync.dma_start(out=factor[:], in_=fk.rearrange("(p t) o -> p (t o)", t=PACK))
+        nc.sync.dma_start(out=w_raw[:].bitcast(I32), in_=w_words[0].bitcast(I32))
+        load_scale_rows(nc.sync, w_plane_raw, w_scales)
+        nc.sync.dma_start(out=wb_codes[:].bitcast(I32), in_=wb_words[0].bitcast(I32))
+        nc.sync.dma_start(out=resid[:], in_=rs.rearrange("(h p) n -> p h n", p=P))
+        load_scale_rows(nc.gpsimd, wb_plane, wb_scales)
+
+        xo_codes = tile("xo_codes", [P, J], U32)
+        xo_picked_plane = tile("xo_picked_plane", [P, J], U8)
+        nc.vector.tensor_copy(xo_codes[:], xo_table[:].bitcast(U32).indirect(list_o[:]))
+        nc.vector.tensor_copy(xo_picked_plane[:], xo_plane[:].indirect(list_o[:]))
+        w2_codes = tile("w2_codes", [P, 2 * R], U8)
+        w2_plane = tile("w2_plane", [P, R], U8)
+        deal_columns(nc, w2_codes[:].bitcast(U16), w2_raw[:].bitcast(U16), 8)
+        deal_columns(nc, w2_plane[:], w2_plane_raw[:], 16)
+
+        def first_stage(bank, codes, plane, moving, moving_plane):
+            for t in range(PACK):
+                nc.tensor.matmul_mx(
+                    out=bank[:, t, :],
+                    lhsT=codes[:, 2 * P * t : 2 * P * (t + 1)].bitcast(E2M1),
+                    lhsT_scale=plane[:, P * t : P * (t + 1)],
+                    rhs=moving,
+                    rhs_scale=moving_plane,
+                    start=True,
+                    stop=True,
+                )
+
+        cols = [slice(HALF * h, HALF * (h + 1)) for h in range(HALVES)]
+        q_banks = [ps.tile([P, PACK, HALF], F32, name="q_bank%d" % h) for h in range(HALVES)]
+        steps = [tile("step%d" % h, [P, HALF, PACK], F32) for h in range(HALVES)]
+        for h in range(HALVES):
+            first_stage(q_banks[h], w2_codes, w2_plane, xo_codes[:, cols[h]].bitcast(E5M2), xo_picked_plane[:, cols[h]])
+
+        picked_a = tile("picked_a", [P, PACK, J], F32)
+        picked_b = tile("picked_b", [P, PACK, J], F32)
+        gap = tile("gap", [P, PACK, J], F32)
+
+        def pick(t):
+            nc.scalar.activation(picked_b[:, t, :], xb_pairs[t // 2][:, t % 2, :].indirect(list_b[:]), ACT.Copy)
+            nc.scalar.activation(picked_a[:, t, :], xa_pairs[t // 2][:, t % 2, :].indirect(list_a[:]), ACT.Copy)
+            nc.vector.scalar_tensor_tensor(
+                out=gap[:, t, :], in0=picked_b[:, t, :], scalar=bound[:, t : t + 1], in1=picked_a[:, t, :],
+                op0=ALU.min, op1=ALU.subtract,
+            )
+
+        pick(0)
+        pick(1)
+        for h in range(HALVES):
+            count = min(HALF, J - 1 - HALF * h)
+            nc.scalar.activation(
+                prev_q[:, HALF * h + 1 : HALF * h + 1 + count, :],
+                q_banks[h][:, :, 0:count].rearrange("p t j -> p j t"),
+                ACT.Copy, scale=-0.6,
+            )
+            nc.vector.tensor_tensor(
+                steps[h][:], q_banks[h][:].rearrange("p t j -> p j t"), prev_q[:, cols[h], :], ALU.add
+            )
+        w_codes = tile("w_codes", [P, 2 * R], U8)
+        w_plane = tile("w_plane", [P, R], U8)
+        deal_columns(nc, w_codes[:].bitcast(U16), w_raw[:].bitcast(U16), 8)
+        deal_columns(nc, w_plane[:], w_plane_raw[:], 16)
+        nc.vector.tensor_scalar(neg_factor[:], factor[:], -1.0, 0.0, ALU.mult, ALU.add)
+        pick(2)
+        pick(3)
+        resid_scaled = tile("resid_scaled", [P, HALVES, N], F32)
+        nc.scalar.activation(resid_scaled[:], resid[:], ACT.Copy, scale=0.3)
+
+        u_round = [tile("u_round%d" % h, [P, HALF * PACK], BF16) for h in range(HALVES)]
+        u_codes = [tile("u_codes%d" % h, [P, HALF], U32) for h in range(HALVES)]
+        u_plane = [tile("u_plane%d" % h, [P, HALF], U8) for h in range(HALVES)]
+        a_banks = [ps.tile([P, PACK, HALF], F32, name="a_bank%d" % h) for h in range(HALVES)]
+        for h in range(HALVES):
+            nc.vector.tensor_tensor(
+                u_round[h][:].rearrange("p (c i t) -> p c t i", t=PACK, i=4),
+                gap[:, :, cols[h]].rearrange("p t (c i) -> p c t i", i=4),
+                neg_factor[:].unsqueeze(1).unsqueeze(3).to_broadcast([P, HALF // 4, PACK, 4]),
+                ALU.mult,
+            )
+        for h in range(HALVES):
+            nc.vector.quantize_mx(out=u_codes[h][:].bitcast(E4M3), scales=u_plane[h][:], in_=u_round[h][:])
+            first_stage(a_banks[h], w_codes, w_plane, u_codes[h][:].bitcast(E4M3), u_plane[h][:])
+
+        hid_round = [tile("hid_round%d" % h, [P, HALF * PACK], BF16) for h in range(HALVES)]
+        hid_codes = [tile("hid_codes%d" % h, [P, HALF], U32) for h in range(HALVES)]
+        hid_plane = [tile("hid_plane%d" % h, [P, HALF], U8) for h in range(HALVES)]
+        p_banks = [ps.tile([P, N], F32, name="p_bank%d" % h) for h in range(HALVES)]
+        for h in range(HALVES):
+            nc.vector.tensor_tensor(
+                hid_round[h][:].rearrange("p (j t) -> p j t", t=PACK),
+                a_banks[h][:].rearrange("p t j -> p j t"), steps[h][:], ALU.max,
+            )
+        for h in range(HALVES):
+            nc.vector.quantize_mx(out=hid_codes[h][:].bitcast(E5M2), scales=hid_plane[h][:], in_=hid_round[h][:])
+            nc.tensor.matmul_mx(
+                out=p_banks[h][:], lhsT=hid_codes[h][:].bitcast(E5M2), lhsT_scale=hid_plane[h][:],
+                rhs=wb_codes[:].bitcast(E2M1), rhs_scale=wb_plane[:], start=True, stop=True,
+            )
+
+        for h in range(HALVES):
+            size = tile("size%d" % h, [P, N], F32)
+            peak = tile("peak%d" % h, [P, 1], F32)
+            denom = tile("denom%d" % h, [P, 1], F32)
+            inv = tile("inv%d" % h, [P, 1], F32)
+            result = tile("result%d" % h, [P, N], F32)
+            nc.scalar.activation(size[:], p_banks[h][:], ACT.Abs)
+            nc.vector.tensor_reduce(peak[:], size[:], mybir.AxisListType.X, ALU.max)
+            nc.vector.tensor_scalar(denom[:], peak[:], 0.2, None, ALU.add)
+            nc.vector.reciprocal(inv[:], denom[:])
+            nc.vector.scalar_tensor_tensor(
+                out=result[:], in0=p_banks[h][:], scalar=inv[:], in1=resid_scaled[:, h, :],
+                op0=ALU.mult, op1=ALU.add,
+            )
+            nc.sync.dma_start(out=out[cols[h], :], in_=result[:])

@@ -71,28 +71,30 @@ def tile_list_two_boundedgaps_other_stepgap_rowpeaks_kernel(
 
         for plane in (xo_plane, w2_plane_raw, w_plane_raw, wb_plane):
             nc.vector.memset(plane[:].bitcast(I32), 0)
-        nc.vector.memset(prev_q[:, 0, :], 0.0)
+        before_first = tile("before_first", [P, PACK], F32)
+        nc.gpsimd.memset(before_first[:], 0.0)
+        nc.scalar.activation(prev_q[:, 0, :], before_first[:], ACT.Copy, scale=-0.6)
 
         xa_rows = xa.rearrange("(p t) c -> p t c", t=PACK)
         xb_rows = xb.rearrange("(p t) c -> p t c", t=PACK)
-        nc.sync.dma_start(list_b[:], offs2)
-        nc.sync.dma_start(out=xb_pairs[0][:], in_=xb_rows[:, 0:2, :])
         nc.sync.dma_start(list_o[:], offs3)
+        nc.sync.dma_start(list_b[:], offs2)
+        load_scale_rows(nc.sync, xo_plane, xo_scales)
         nc.sync.dma_start(out=xo_table[:], in_=xo_words[0].rearrange("p n t -> p (n t)").bitcast(I32))
-        load_scale_rows(nc.scalar, xo_plane, xo_scales)
-        nc.sync.dma_start(list_a[:], offs)
-        nc.sync.dma_start(out=xa_pairs[0][:], in_=xa_rows[:, 0:2, :])
+        nc.sync.dma_start(out=xb_pairs[0][:], in_=xb_rows[:, 0:2, :])
         nc.sync.dma_start(out=w2_raw[:].bitcast(I32), in_=w2_words[0].bitcast(I32))
         load_scale_rows(nc.sync, w2_plane_raw, w2_scales)
-        nc.sync.dma_start(out=bound[:], in_=hb.rearrange("(p t) o -> p (t o)", t=PACK))
+        nc.sync.dma_start(out=xa_pairs[0][:], in_=xa_rows[:, 0:2, :])
+        nc.sync.dma_start(list_a[:], offs)
         nc.sync.dma_start(out=xb_pairs[1][:], in_=xb_rows[:, 2:4, :])
-        nc.sync.dma_start(out=xa_pairs[1][:], in_=xa_rows[:, 2:4, :])
-        nc.sync.dma_start(out=factor[:], in_=fk.rearrange("(p t) o -> p (t o)", t=PACK))
         nc.sync.dma_start(out=w_raw[:].bitcast(I32), in_=w_words[0].bitcast(I32))
         load_scale_rows(nc.sync, w_plane_raw, w_scales)
+        nc.sync.dma_start(out=xa_pairs[1][:], in_=xa_rows[:, 2:4, :])
         nc.sync.dma_start(out=wb_codes[:].bitcast(I32), in_=wb_words[0].bitcast(I32))
         nc.sync.dma_start(out=resid[:], in_=rs.rearrange("(h p) n -> p h n", p=P))
-        load_scale_rows(nc.gpsimd, wb_plane, wb_scales)
+        load_scale_rows(nc.sync, wb_plane, wb_scales)
+        nc.gpsimd.dma_start(out=bound[:], in_=hb.rearrange("(p t) o -> p (t o)", t=PACK))
+        nc.gpsimd.dma_start(out=factor[:], in_=fk.rearrange("(p t) o -> p (t o)", t=PACK))
 
         xo_codes = tile("xo_codes", [P, J], U32)
         xo_picked_plane = tile("xo_picked_plane", [P, J], U8)
@@ -125,16 +127,26 @@ def tile_list_two_boundedgaps_other_stepgap_rowpeaks_kernel(
         picked_b = tile("picked_b", [P, PACK, J], F32)
         gap = tile("gap", [P, PACK, J], F32)
 
-        def pick(t):
-            nc.scalar.activation(picked_b[:, t, :], xb_pairs[t // 2][:, t % 2, :].indirect(list_b[:]), ACT.Copy)
-            nc.scalar.activation(picked_a[:, t, :], xa_pairs[t // 2][:, t % 2, :].indirect(list_a[:]), ACT.Copy)
+        def pick(engine, picked, pairs, offsets, t, part):
+            window = pairs[t // 2][:, t % 2, :].indirect(offsets[:, part.start // 16 : part.stop // 16])
+            if engine == "vector":
+                nc.vector.tensor_copy(picked[:, t, part], window)
+            else:
+                nc.scalar.activation(picked[:, t, part], window, ACT.Copy)
+
+        def bounded_gap(t, part):
             nc.vector.scalar_tensor_tensor(
-                out=gap[:, t, :], in0=picked_b[:, t, :], scalar=bound[:, t : t + 1], in1=picked_a[:, t, :],
+                out=gap[:, t, part], in0=picked_b[:, t, part], scalar=bound[:, t : t + 1], in1=picked_a[:, t, part],
                 op0=ALU.min, op1=ALU.subtract,
             )
 
-        pick(0)
-        pick(1)
+        every = slice(0, J)
+        pick("scalar", picked_b, xb_pairs, list_b, 0, every)
+        pick("scalar", picked_b, xb_pairs, list_b, 1, every)
+        pick("scalar", picked_a, xa_pairs, list_a, 0, every)
+        pick("vector", picked_a, xa_pairs, list_a, 1, every)
+        bounded_gap(1, every)
+        bounded_gap(0, every)
         for h in range(HALVES):
             count = min(HALF, J - 1 - HALF * h)
             nc.scalar.activation(
@@ -145,13 +157,15 @@ def tile_list_two_boundedgaps_other_stepgap_rowpeaks_kernel(
             nc.vector.tensor_tensor(
                 steps[h][:], q_banks[h][:].rearrange("p t j -> p j t"), prev_q[:, cols[h], :], ALU.add
             )
+            pick("scalar", picked_b, xb_pairs, list_b, 2 + h, every)
         w_codes = tile("w_codes", [P, 2 * R], U8)
         w_plane = tile("w_plane", [P, R], U8)
         deal_columns(nc, w_codes[:].bitcast(U16), w_raw[:].bitcast(U16), 8)
         deal_columns(nc, w_plane[:], w_plane_raw[:], 16)
-        nc.vector.tensor_scalar(neg_factor[:], factor[:], -1.0, 0.0, ALU.mult, ALU.add)
-        pick(2)
-        pick(3)
+        nc.gpsimd.tensor_scalar(neg_factor[:], factor[:], -1.0, 0.0, ALU.mult, ALU.add)
+        for h in range(HALVES):
+            pick("scalar", picked_a, xa_pairs, list_a, 2, cols[h])
+            pick("vector" if h == 0 else "scalar", picked_a, xa_pairs, list_a, 3, cols[h])
         resid_scaled = tile("resid_scaled", [P, HALVES, N], F32)
         nc.scalar.activation(resid_scaled[:], resid[:], ACT.Copy, scale=0.3)
 
@@ -159,16 +173,27 @@ def tile_list_two_boundedgaps_other_stepgap_rowpeaks_kernel(
         u_codes = [tile("u_codes%d" % h, [P, HALF], U32) for h in range(HALVES)]
         u_plane = [tile("u_plane%d" % h, [P, HALF], U8) for h in range(HALVES)]
         a_banks = [ps.tile([P, PACK, HALF], F32, name="a_bank%d" % h) for h in range(HALVES)]
-        for h in range(HALVES):
+
+        def scale_and_round(h):
             nc.vector.tensor_tensor(
                 u_round[h][:].rearrange("p (c i t) -> p c t i", t=PACK, i=4),
                 gap[:, :, cols[h]].rearrange("p t (c i) -> p c t i", i=4),
                 neg_factor[:].unsqueeze(1).unsqueeze(3).to_broadcast([P, HALF // 4, PACK, 4]),
                 ALU.mult,
             )
-        for h in range(HALVES):
+
+        def multiply_u(h):
             nc.vector.quantize_mx(out=u_codes[h][:].bitcast(E4M3), scales=u_plane[h][:], in_=u_round[h][:])
             first_stage(a_banks[h], w_codes, w_plane, u_codes[h][:].bitcast(E4M3), u_plane[h][:])
+
+        bounded_gap(3, cols[0])
+        bounded_gap(2, cols[0])
+        scale_and_round(0)
+        bounded_gap(2, cols[1])
+        multiply_u(0)
+        bounded_gap(3, cols[1])
+        scale_and_round(1)
+        multiply_u(1)
 
         hid_round = [tile("hid_round%d" % h, [P, HALF * PACK], BF16) for h in range(HALVES)]
         hid_codes = [tile("hid_codes%d" % h, [P, HALF], U32) for h in range(HALVES)]
@@ -179,7 +204,6 @@ def tile_list_two_boundedgaps_other_stepgap_rowpeaks_kernel(
                 hid_round[h][:].rearrange("p (j t) -> p j t", t=PACK),
                 a_banks[h][:].rearrange("p t j -> p j t"), steps[h][:], ALU.max,
             )
-        for h in range(HALVES):
             nc.vector.quantize_mx(out=hid_codes[h][:].bitcast(E5M2), scales=hid_plane[h][:], in_=hid_round[h][:])
             nc.tensor.matmul_mx(
                 out=p_banks[h][:], lhsT=hid_codes[h][:].bitcast(E5M2), lhsT_scale=hid_plane[h][:],
@@ -188,13 +212,12 @@ def tile_list_two_boundedgaps_other_stepgap_rowpeaks_kernel(
 
         for h in range(HALVES):
             size = tile("size%d" % h, [P, N], F32)
-            peak = tile("peak%d" % h, [P, 1], F32)
+            shifted = tile("shifted%d" % h, [P, N], F32)
             denom = tile("denom%d" % h, [P, 1], F32)
             inv = tile("inv%d" % h, [P, 1], F32)
             result = tile("result%d" % h, [P, N], F32)
             nc.scalar.activation(size[:], p_banks[h][:], ACT.Abs)
-            nc.vector.tensor_reduce(peak[:], size[:], mybir.AxisListType.X, ALU.max)
-            nc.vector.tensor_scalar(denom[:], peak[:], 0.2, None, ALU.add)
+            nc.vector.tensor_scalar(shifted[:], size[:], 0.2, None, ALU.add, ALU.max, accum_out=denom[:])
             nc.vector.reciprocal(inv[:], denom[:])
             nc.vector.scalar_tensor_tensor(
                 out=result[:], in0=p_banks[h][:], scalar=inv[:], in1=resid_scaled[:, h, :],

from contextlib import ExitStack

import concourse.mybir as mybir

K, T, J, S, R, F, Z, N = 512, 512, 256, 512, 512, 512, 1024, 256
FLOPS = 2 * K * R * J + 2 * F * R * J + 2 * R * J * N

F32 = mybir.dt.float32
BF16 = mybir.dt.bfloat16
I32 = mybir.dt.int32
U32 = mybir.dt.uint32
U16 = mybir.dt.uint16
U8 = mybir.dt.uint8
E4M3 = mybir.dt.float8_e4m3fn_x4
E5M2 = mybir.dt.float8_e5m2_x4
E2M1 = mybir.dt.float4_e2m1fn_x4
ALU = mybir.AluOpType
ACT = mybir.ActivationFunctionType

P = 128
PACK = 4
HALF = 128
HALVES = J // HALF


def load_scale_rows(queue, plane, scales):
    for quad in range(4):
        queue.dma_start(
            out=plane[32 * quad : 32 * quad + 4, :].bitcast(I32),
            in_=scales[0, 4 * quad : 4 * quad + 4, :].bitcast(I32),
        )


def deal_columns(nc, dealt, raw, run):
    nc.vector.tensor_copy(
        out=dealt.rearrange("p (t c i) -> p c t i", t=PACK, i=run),
        in_=raw.rearrange("p (c i t) -> p c t i", t=PACK, i=run),
    )


def tile_list_two_boundedgaps_other_stepgap_rowpeaks_kernel(
    tc, xa, xb, hb, fk, w_words, w_scales, xo_words, xo_scales, w2_words, w2_scales,
    wb_words, wb_scales, rs, offs, offs2, offs3, out,
):
    nc = tc.nc
    with ExitStack() as ctx:
        sb = ctx.enter_context(tc.tile_pool(name="sb", bufs=1))
        ps = ctx.enter_context(tc.psum_pool(name="ps", bufs=1))

        def tile(name, shape, dtype):
            return sb.tile(shape, dtype, name=name, align_bytes=64)

        list_a = tile("list_a", [P, J // 16], U16)
        list_b = tile("list_b", [P, J // 16], U16)
        list_o = tile("list_o", [P, J // 16], U16)
        xo_table = tile("xo_table", [P, Z], I32)
        xo_plane = tile("xo_plane", [P, Z], U8)
        w_raw = tile("w_raw", [P, 2 * R], U8)
        w_plane_raw = tile("w_plane_raw", [P, R], U8)
        w2_raw = tile("w2_raw", [P, 2 * R], U8)
        w2_plane_raw = tile("w2_plane_raw", [P, R], U8)
        wb_codes = tile("wb_codes", [P, 2 * N], U8)
        wb_plane = tile("wb_plane", [P, N], U8)
        xa_pairs = [tile("xa_pair%d" % i, [P, 2, T], F32) for i in range(2)]
        xb_pairs = [tile("xb_pair%d" % i, [P, 2, S], F32) for i in range(2)]
        bound = tile("bound", [P, PACK], F32)
        factor = tile("factor", [P, PACK], F32)
        neg_factor = tile("neg_factor", [P, PACK], F32)
        resid = tile("resid", [P, HALVES, N], F32)
        prev_q = tile("prev_q", [P, J, PACK], F32)

        for plane in (xo_plane, w2_plane_raw, w_plane_raw, wb_plane):
            nc.vector.memset(plane[:].bitcast(I32), 0)
        before_first = tile("before_first", [P, PACK], F32)
        nc.gpsimd.memset(before_first[:], 0.0)
        nc.scalar.activation(prev_q[:, 0, :], before_first[:], ACT.Copy, scale=-0.6)

        xa_rows = xa.rearrange("(p t) c -> p t c", t=PACK)
        xb_rows = xb.rearrange("(p t) c -> p t c", t=PACK)
        nc.sync.dma_start(list_o[:], offs3)
        nc.sync.dma_start(list_b[:], offs2)
        load_scale_rows(nc.sync, xo_plane, xo_scales)
        nc.sync.dma_start(out=xo_table[:], in_=xo_words[0].rearrange("p n t -> p (n t)").bitcast(I32))
        nc.sync.dma_start(out=xb_pairs[0][:], in_=xb_rows[:, 0:2, :])
        nc.sync.dma_start(out=w2_raw[:].bitcast(I32), in_=w2_words[0].bitcast(I32))
        load_scale_rows(nc.sync, w2_plane_raw, w2_scales)
        nc.sync.dma_start(out=xa_pairs[0][:], in_=xa_rows[:, 0:2, :])
        nc.sync.dma_start(list_a[:], offs)
        nc.sync.dma_start(out=xb_pairs[1][:], in_=xb_rows[:, 2:4, :])
        nc.sync.dma_start(out=w_raw[:].bitcast(I32), in_=w_words[0].bitcast(I32))
        load_scale_rows(nc.sync, w_plane_raw, w_scales)
        nc.sync.dma_start(out=xa_pairs[1][:], in_=xa_rows[:, 2:4, :])
        nc.sync.dma_start(out=wb_codes[:].bitcast(I32), in_=wb_words[0].bitcast(I32))
        nc.sync.dma_start(out=resid[:], in_=rs.rearrange("(h p) n -> p h n", p=P))
        load_scale_rows(nc.sync, wb_plane, wb_scales)
        nc.gpsimd.dma_start(out=bound[:], in_=hb.rearrange("(p t) o -> p (t o)", t=PACK))
        nc.gpsimd.dma_start(out=factor[:], in_=fk.rearrange("(p t) o -> p (t o)", t=PACK))

        xo_codes = tile("xo_codes", [P, J], U32)
        xo_picked_plane = tile("xo_picked_plane", [P, J], U8)
        nc.vector.tensor_copy(xo_codes[:], xo_table[:].bitcast(U32).indirect(list_o[:]))
        nc.vector.tensor_copy(xo_picked_plane[:], xo_plane[:].indirect(list_o[:]))
        w2_codes = tile("w2_codes", [P, 2 * R], U8)
        w2_plane = tile("w2_plane", [P, R], U8)
        deal_columns(nc, w2_codes[:].bitcast(U16), w2_raw[:].bitcast(U16), 8)
        deal_columns(nc, w2_plane[:], w2_plane_raw[:], 16)

        def first_stage(bank, codes, plane, moving, moving_plane):
            for t in range(PACK):
                nc.tensor.matmul_mx(
                    out=bank[:, t, :],
                    lhsT=codes[:, 2 * P * t : 2 * P * (t + 1)].bitcast(E2M1),
                    lhsT_scale=plane[:, P * t : P * (t + 1)],
                    rhs=moving,
                    rhs_scale=moving_plane,
                    start=True,
                    stop=True,
                )

        cols = [slice(HALF * h, HALF * (h + 1)) for h in range(HALVES)]
        q_banks = [ps.tile([P, PACK, HALF], F32, name="q_bank%d" % h) for h in range(HALVES)]
        steps = [tile("step%d" % h, [P, HALF, PACK], F32) for h in range(HALVES)]
        for h in range(HALVES):
            first_stage(q_banks[h], w2_codes, w2_plane, xo_codes[:, cols[h]].bitcast(E5M2), xo_picked_plane[:, cols[h]])

        picked_a = tile("picked_a", [P, PACK, J], F32)
        picked_b = tile("picked_b", [P, PACK, J], F32)
        gap = tile("gap", [P, PACK, J], F32)

        def pick(engine, picked, pairs, offsets, t, part):
            window = pairs[t // 2][:, t % 2, :].indirect(offsets[:, part.start // 16 : part.stop // 16])
            if engine == "vector":
                nc.vector.tensor_copy(picked[:, t, part], window)
            else:
                nc.scalar.activation(picked[:, t, part], window, ACT.Copy)

        def bounded_gap(t, part):
            nc.vector.scalar_tensor_tensor(
                out=gap[:, t, part], in0=picked_b[:, t, part], scalar=bound[:, t : t + 1], in1=picked_a[:, t, part],
                op0=ALU.min, op1=ALU.subtract,
            )

        every = slice(0, J)
        pick("scalar", picked_b, xb_pairs, list_b, 0, every)
        pick("scalar", picked_b, xb_pairs, list_b, 1, every)
        pick("scalar", picked_a, xa_pairs, list_a, 0, every)
        pick("vector", picked_a, xa_pairs, list_a, 1, every)
        bounded_gap(1, every)
        bounded_gap(0, every)
        for h in range(HALVES):
            count = min(HALF, J - 1 - HALF * h)
            nc.scalar.activation(
                prev_q[:, HALF * h + 1 : HALF * h + 1 + count, :],
                q_banks[h][:, :, 0:count].rearrange("p t j -> p j t"),
                ACT.Copy, scale=-0.6,
            )
            nc.vector.tensor_tensor(
                steps[h][:], q_banks[h][:].rearrange("p t j -> p j t"), prev_q[:, cols[h], :], ALU.add
            )
            pick("scalar", picked_b, xb_pairs, list_b, 2 + h, every)
        w_codes = tile("w_codes", [P, 2 * R], U8)
        w_plane = tile("w_plane", [P, R], U8)
        deal_columns(nc, w_codes[:].bitcast(U16), w_raw[:].bitcast(U16), 8)
        deal_columns(nc, w_plane[:], w_plane_raw[:], 16)
        nc.gpsimd.tensor_scalar(neg_factor[:], factor[:], -1.0, 0.0, ALU.mult, ALU.add)
        for h in range(HALVES):
            pick("scalar", picked_a, xa_pairs, list_a, 2, cols[h])
            pick("vector" if h == 0 else "scalar", picked_a, xa_pairs, list_a, 3, cols[h])
        resid_scaled = tile("resid_scaled", [P, HALVES, N], F32)
        nc.scalar.activation(resid_scaled[:], resid[:], ACT.Copy, scale=0.3)

        u_round = [tile("u_round%d" % h, [P, HALF * PACK], BF16) for h in range(HALVES)]
        u_codes = [tile("u_codes%d" % h, [P, HALF], U32) for h in range(HALVES)]
        u_plane = [tile("u_plane%d" % h, [P, HALF], U8) for h in range(HALVES)]
        a_banks = [ps.tile([P, PACK, HALF], F32, name="a_bank%d" % h) for h in range(HALVES)]

        def scale_and_round(h):
            nc.vector.tensor_tensor(
                u_round[h][:].rearrange("p (c i t) -> p c t i", t=PACK, i=4),
                gap[:, :, cols[h]].rearrange("p t (c i) -> p c t i", i=4),
                neg_factor[:].unsqueeze(1).unsqueeze(3).to_broadcast([P, HALF // 4, PACK, 4]),
                ALU.mult,
            )

        def multiply_u(h):
            nc.vector.quantize_mx(out=u_codes[h][:].bitcast(E4M3), scales=u_plane[h][:], in_=u_round[h][:])
            first_stage(a_banks[h], w_codes, w_plane, u_codes[h][:].bitcast(E4M3), u_plane[h][:])

        bounded_gap(3, cols[0])
        bounded_gap(2, cols[0])
        scale_and_round(0)
        bounded_gap(2, cols[1])
        multiply_u(0)
        bounded_gap(3, cols[1])
        scale_and_round(1)
        multiply_u(1)

        hid_round = [tile("hid_round%d" % h, [P, HALF * PACK], BF16) for h in range(HALVES)]
        hid_codes = [tile("hid_codes%d" % h, [P, HALF], U32) for h in range(HALVES)]
        hid_plane = [tile("hid_plane%d" % h, [P, HALF], U8) for h in range(HALVES)]
        p_banks = [ps.tile([P, N], F32, name="p_bank%d" % h) for h in range(HALVES)]
        for h in range(HALVES):
            nc.vector.tensor_tensor(
                hid_round[h][:].rearrange("p (j t) -> p j t", t=PACK),
                a_banks[h][:].rearrange("p t j -> p j t"), steps[h][:], ALU.max,
            )
            nc.vector.quantize_mx(out=hid_codes[h][:].bitcast(E5M2), scales=hid_plane[h][:], in_=hid_round[h][:])
            nc.tensor.matmul_mx(
                out=p_banks[h][:], lhsT=hid_codes[h][:].bitcast(E5M2), lhsT_scale=hid_plane[h][:],
                rhs=wb_codes[:].bitcast(E2M1), rhs_scale=wb_plane[:], start=True, stop=True,
            )

        for h in range(HALVES):
            size = tile("size%d" % h, [P, N], F32)
            shifted = tile("shifted%d" % h, [P, N], F32)
            denom = tile("denom%d" % h, [P, 1], F32)
            inv = tile("inv%d" % h, [P, 1], F32)
            result = tile("result%d" % h, [P, N], F32)
            nc.scalar.activation(size[:], p_banks[h][:], ACT.Abs)
            nc.vector.tensor_scalar(shifted[:], size[:], 0.2, None, ALU.add, ALU.max, accum_out=denom[:])
            nc.vector.reciprocal(inv[:], denom[:])
            nc.vector.scalar_tensor_tensor(
                out=result[:], in0=p_banks[h][:], scalar=inv[:], in1=resid_scaled[:, h, :],
                op0=ALU.mult, op1=ALU.add,
            )
            nc.sync.dma_start(out=out[cols[h], :], in_=result[:])
